import numpy as np
import ml_dtypes


def mxq(x, axis, fmt="e4m3"):
    dtype, down = {"e4m3": (ml_dtypes.float8_e4m3fn, 7), "e5m2": (ml_dtypes.float8_e5m2, 14)}[fmt]
    v = np.moveaxis(np.asarray(x, np.float32).astype(ml_dtypes.bfloat16).astype(np.float64), axis, -1)
    blocks = v.reshape(v.shape[:-1] + (-1, 32))
    amax = np.abs(blocks).max(-1, keepdims=True)
    byte = np.maximum(np.where(amax > 0, np.frexp(amax)[1] - 1 + 127, 0) - down, 1)
    scale = np.exp2(byte - 127.0)
    codes = (blocks / scale).astype(np.float32).astype(dtype).astype(np.float64)
    return np.moveaxis((codes * scale).reshape(v.shape), -1, axis)


WIDE = False


def mx_kscale(k):
    if not WIDE:
        return np.ones(k)
    levels = np.array([30, -30])
    if k % 512:
        return np.exp2(np.random.permutation(np.resize(levels, k // 32))).repeat(32)
    a = np.empty((k // 512, 16))
    for p in range(k // 512):
        a[p, :8] = np.random.permutation(np.resize(levels, 8))
        for g in range(8):
            far = levels[np.abs(levels - a[p, g]) >= 10]
            a[p, g + 8] = far[np.random.randint(len(far))]
    return np.exp2(a.ravel()).repeat(32)


def f64(x):
    return np.asarray(x).astype(np.float64)


def striped(idx):
    return np.tile(np.asarray(idx).reshape(-1, 16).T, (8, 1)).astype(np.uint16)


def unstriped(offs):
    return offs[:16].T.reshape(-1).astype(np.int64)


E2M1 = np.array([0.0, 0.5, 1.0, 1.5, 2.0, 3.0, 4.0, 6.0, -0.0, -0.5, -1.0, -1.5, -2.0, -3.0, -4.0, -6.0])


def pack_weight(w, fmt):
    k, n = w.shape
    w = f64(np.asarray(w, np.float32).astype(ml_dtypes.bfloat16)).reshape(k // 32, 32, n)
    amax = np.abs(w).max(1)
    if fmt in ("e4m3", "e5m2"):
        byte = np.frexp(amax)[1] - 1 + 127 - (7 if fmt == "e4m3" else 14)
    else:
        mant, ex = np.frexp(amax / 6.0)
        byte = np.where(mant > 0.5, ex, ex - 1) + 127
    byte = np.clip(np.where(amax > 0, byte, 1), 1, 254)
    scaled = (w * np.exp2(127.0 - byte)[:, None, :]).reshape(k, n).astype(np.float32)
    by_word = np.ascontiguousarray(scaled.reshape(k // 512, 128, 4, n).transpose(0, 1, 3, 2))
    if fmt in ("e4m3", "e5m2"):
        words = by_word.astype(ml_dtypes.float8_e4m3fn if fmt == "e4m3" else ml_dtypes.float8_e5m2).view(np.uint8)
    else:
        c = by_word.astype(ml_dtypes.float4_e2m1fn).view(np.uint8) & 0xF
        words = (c[..., 0::2] | (c[..., 1::2] << 4)).reshape(k // 512, 128, 2 * n)
    return np.ascontiguousarray(words), np.ascontiguousarray(byte.astype(np.uint8).reshape(k // 512, 16, n))


def unpack_weight(words, scales, fmt):
    g, _, n = scales.shape
    words = np.ascontiguousarray(words).reshape(g, 128, n, -1)
    if fmt in ("e4m3", "e5m2"):
        vals = words.view(ml_dtypes.float8_e4m3fn if fmt == "e4m3" else ml_dtypes.float8_e5m2).astype(np.float64)
    else:
        nib = np.empty((g, 128, n, 4), np.uint8)
        nib[..., 0::2] = words & 0xF
        nib[..., 1::2] = words >> 4
        vals = E2M1[nib]
    vals = vals * np.repeat(np.exp2(scales.astype(np.float64) - 127.0), 8, axis=1)[..., None]
    return vals.transpose(0, 1, 3, 2).reshape(g * 512, n)


K, T, J, R, V, O, N, E = 512, 1024, 256, 512, 1024, 128, 256, 512


def setup_inputs():
    n = np.random.standard_normal
    idx = np.random.permutation(V)[:R]
    idx2 = np.random.permutation(T)[:J]
    idx3 = np.random.permutation(J)[:O]
    idx4 = np.random.permutation(J)[:O]
    idx5 = np.random.permutation(E)[:O]
    idx6 = np.random.permutation(E)[:O]
    fk = mx_kscale(K)
    fr = mx_kscale(R)
    tr = np.ones(V)
    tr[idx] = fr
    xtp = pack_weight(n((K, T)) / fk[:, None], "e4m3")
    wtp = pack_weight(n((K, V)) * 1 / np.sqrt(K) * fk[:, None] * tr, "e2m1")
    w2p = pack_weight(n((K, R)) * 1 / np.sqrt(K) * fk[:, None], "e5m2")
    wbp = pack_weight(n((R, N)) * 1 / np.sqrt(R) / fr[:, None], "e5m2")
    return {
        "xt_words": xtp[0],
        "xt_scales": xtp[1],
        "wt_words": wtp[0],
        "wt_scales": wtp[1],
        "w2_words": w2p[0],
        "w2_scales": w2p[1],
        "wb_words": wbp[0],
        "wb_scales": wbp[1],
        "offs": striped(idx),
        "offs2": striped(idx2),
        "offs3": striped(idx3),
        "offs4": striped(idx4),
        "offs5": striped(idx5),
        "offs6": striped(idx6),
    }


def reference(xt_words, xt_scales, wt_words, wt_scales, w2_words, w2_scales, wb_words, wb_scales, offs, offs2, offs3, offs4, offs5, offs6):
    idx = unstriped(offs)
    idx2 = unstriped(offs2)
    idx3 = unstriped(offs3)
    idx4 = unstriped(offs4)
    idx5 = unstriped(offs5)
    idx6 = unstriped(offs6)
    xtu = unpack_weight(xt_words, xt_scales, "e4m3")
    wtu = unpack_weight(wt_words, wt_scales, "e2m1")
    w2u = unpack_weight(w2_words, w2_scales, "e5m2")
    wbu = unpack_weight(wb_words, wb_scales, "e5m2")
    wtidxg = wtu[:, idx]
    xtidx2g = xtu[:, idx2]
    a = wtidxg.T @ xtidx2g
    b = w2u.T @ xtidx2g
    lb = b[:, 0:1]
    la = a[:, 0:1]
    hid = np.abs(a[:, idx3] * lb - b[:, idx4] * la)
    hidq = mxq(hid, 0, "e4m3")
    p = wbu.T @ hidq
    pa = np.zeros((N, E))
    pa[:, idx5] = p
    pb = np.zeros((N, E))
    pb[:, idx6] = p
    y = pa + pb
    return y

@@ -1,0 +1,152 @@
+from contextlib import ExitStack
+
+import concourse.mybir as mybir
+
+K, T, J, R, V, O, N, E = 512, 1024, 256, 512, 1024, 128, 256, 512
+FLOPS = 2 * (2 * K * R * J + R * N * O)
+
+F32 = mybir.dt.float32
+BF16 = mybir.dt.bfloat16
+I32 = mybir.dt.int32
+U32 = mybir.dt.uint32
+U16 = mybir.dt.uint16
+U8 = mybir.dt.uint8
+E4M3 = mybir.dt.float8_e4m3fn_x4
+E5M2 = mybir.dt.float8_e5m2_x4
+E2M1 = mybir.dt.float4_e2m1fn_x4
+ALU = mybir.AluOpType
+ACT = mybir.ActivationFunctionType
+
+P = 128
+PACK = 4
+QUADS = 4
+
+
+def tile_list_leadboth_storeleads_one_pagetwice_kernel(
+    tc, xt_words, xt_scales, wt_words, wt_scales, w2_words, w2_scales, wb_words, wb_scales,
+    offs, offs2, offs3, offs4, offs5, offs6, out,
+):
+    nc = tc.nc
+    with ExitStack() as ctx:
+        sb = ctx.enter_context(tc.tile_pool(name="sb", bufs=1))
+        ps = ctx.enter_context(tc.psum_pool(name="ps", bufs=1))
+
+        def load_list(src, name):
+            tile = sb.tile([P, src.shape[1]], U16, name=name)
+            nc.sync.dma_start(tile[:], src)
+            return tile
+
+        def load_words(src, cols, dtype, name):
+            tile = sb.tile([P, cols], dtype, name=name, align_bytes=64)
+            nc.sync.dma_start(tile[:].bitcast(I32), src.bitcast(I32))
+            return tile
+
+        def zeroed_scales(cols, name):
+            tile = sb.tile([P, cols], U8, name=name, align_bytes=64)
+            nc.vector.memset(tile[:].bitcast(I32), 0)
+            return tile
+
+        def load_scales(tile, src):
+            for q in range(QUADS):
+                nc.sync.dma_start(tile[32 * q : 32 * q + 4, :].bitcast(I32), src[0, 4 * q : 4 * q + 4, :].bitcast(I32))
+
+        xt_s = zeroed_scales(T, "xt_s")
+        w2_s = zeroed_scales(R, "w2_s")
+        wt_s = zeroed_scales(V, "wt_s")
+        wb_s = zeroed_scales(N, "wb_s")
+
+        wt_w = load_words(wt_words[0], V, U16, "wt_w")
+        w2_rows = sb.tile([4, QUADS, R // 4], I32, name="w2_rows")
+        nc.sync.dma_start(w2_rows[:], w2_scales[0].bitcast(I32).rearrange("(q r) c -> r q c", r=4))
+        list1 = load_list(offs, "list1")
+        list2 = load_list(offs2, "list2")
+        xt_w = load_words(xt_words[0].rearrange("p c r -> p (c r)"), T, U32, "xt_w")
+        load_scales(xt_s, xt_scales)
+        w2_w = load_words(w2_words[0].rearrange("p c r -> p (c r)"), R, U32, "w2_w")
+        load_scales(wt_s, wt_scales)
+        list3 = load_list(offs3, "list3")
+        list4 = load_list(offs4, "list4")
+        wb_w = load_words(wb_words[0].rearrange("p c r -> p (c r)"), N, U32, "wb_w")
+        load_scales(wb_s, wb_scales)
+        list5 = load_list(offs5, "list5")
+        list6 = load_list(offs6, "list6")
+
+        pages = {}
+        for h in range(N // P):
+            for which in "ab":
+                page = sb.tile([P, E], F32, name="page_%s%d" % (which, h))
+                nc.vector.memset(page[:], 0.0)
+                pages[which, h] = page
+
+        for q in range(QUADS):
+            nc.vector.tensor_copy(w2_s[32 * q : 32 * q + 4, :].bitcast(I32), w2_rows[:, q, :])
+
+        wt_g = sb.tile([P, R], U16, name="wt_g")
+        nc.vector.tensor_copy(wt_g[:], wt_w[:].indirect(list1[:]))
+        wt_d = sb.tile([P, R], U16, name="wt_d", align_bytes=64)
+        nc.vector.tensor_copy(wt_d[:].rearrange("p (t m) -> p t m", t=PACK), wt_g[:].rearrange("p (m t) -> p t m", t=PACK))
+        xt_g = sb.tile([P, J], U32, name="xt_g", align_bytes=64)
+        nc.vector.tensor_copy(xt_g[:], xt_w[:].indirect(list2[:]))
+        xt_gs = sb.tile([P, J], U8, name="xt_gs", align_bytes=64)
+        nc.vector.tensor_copy(xt_gs[:], xt_s[:].indirect(list2[:]))
+
+        w2_d = sb.tile([P, R], U32, name="w2_d", align_bytes=64)
+        nc.scalar.copy(w2_d[:].rearrange("p (t m) -> p t m", t=PACK), w2_w[:].rearrange("p (m t) -> p t m", t=PACK))
+        w2_ds = sb.tile([P, R], U8, name="w2_ds", align_bytes=64)
+        nc.gpsimd.tensor_copy(w2_ds[:].rearrange("p (t m) -> p t m", t=PACK), w2_s[:].rearrange("p (m t) -> p t m", t=PACK))
+
+        wt_ds = sb.tile([P, R], U8, name="wt_ds", align_bytes=64)
+        nc.vector.tensor_copy(wt_ds[:].rearrange("p (t m) -> p m t", t=PACK), wt_s[:].indirect(list1[:]))
+
+        b_rows = []
+        for t in range(PACK):
+            cols = slice(t * P, (t + 1) * P)
+            acc = ps.tile([P, J], F32, name="acc_b%d" % t)
+            nc.tensor.matmul_mx(out=acc[:], lhsT=w2_d[:, cols].bitcast(E5M2), lhsT_scale=w2_ds[:, cols],
+                                rhs=xt_g[:].bitcast(E4M3), rhs_scale=xt_gs[:], start=True, stop=True)
+            rows = sb.tile([P, J], F32, name="b_rows%d" % t)
+            nc.scalar.activation(rows[:], acc[:], ACT.Copy)
+            b_rows.append(rows)
+
+        first = sb.tile([P, PACK, O], F32, name="first")
+        second = sb.tile([P, PACK, O], F32, name="second")
+        diff = sb.tile([P, PACK, O], F32, name="diff")
+        a_rows = []
+        for t in range(PACK):
+            cols = slice(t * P, (t + 1) * P)
+            acc = ps.tile([P, J], F32, name="acc_a%d" % t)
+            nc.tensor.matmul_mx(out=acc[:], lhsT=wt_d[:, cols].bitcast(E2M1), lhsT_scale=wt_ds[:, cols],
+                                rhs=xt_g[:].bitcast(E4M3), rhs_scale=xt_gs[:], start=True, stop=True)
+            rows = sb.tile([P, J], F32, name="a_rows%d" % t)
+            nc.vector.tensor_copy(rows[:], acc[:])
+            a_rows.append(rows)
+        for t in range(PACK):
+            nc.scalar.activation(first[:, t, :], a_rows[t][:].indirect(list3[:]), ACT.Copy, scale=b_rows[t][:, 0:1])
+            nc.scalar.activation(second[:, t, :], b_rows[t][:].indirect(list4[:]), ACT.Copy, scale=a_rows[t][:, 0:1])
+            nc.vector.tensor_tensor(diff[:, t, :], first[:, t, :], second[:, t, :], ALU.subtract)
+
+        hid = sb.tile([P, O, PACK], BF16, name="hid", align_bytes=64)
+        by_place = diff[:].rearrange("p t o -> p o t")
+        nc.vector.scalar_tensor_tensor(hid[:], by_place, -1.0, by_place, ALU.mult, ALU.max)
+        hid_w = sb.tile([P, O], U32, name="hid_w", align_bytes=64)
+        hid_s = sb.tile([P, O], U8, name="hid_s", align_bytes=64)
+        nc.vector.quantize_mx(out=hid_w[:].bitcast(E4M3), scales=hid_s[:], in_=hid[:].rearrange("p o t -> p (o t)"))
+
+        p_rows = []
+        for h in range(N // P):
+            cols = slice(h * P, (h + 1) * P)
+            acc = ps.tile([P, J], F32, name="acc_b%d" % h)
+            nc.tensor.matmul_mx(out=acc[:, 0:O], lhsT=wb_w[:, cols].bitcast(E5M2), lhsT_scale=wb_s[:, cols],
+                                rhs=hid_w[:].bitcast(E4M3), rhs_scale=hid_s[:], start=True, stop=True)
+            rows = sb.tile([P, O], F32, name="p_rows%d" % h)
+            if h == 0:
+                nc.vector.tensor_copy(rows[:], acc[:, 0:O])
+            else:
+                nc.scalar.copy(rows[:], acc[:, 0:O])
+            p_rows.append(rows)
+        for h in range(N // P):
+            nc.vector.tensor_copy(pages["a", h][:].indirect(list5[:]), p_rows[h][:])
+            nc.scalar.activation(pages["b", h][:].indirect(list6[:]), p_rows[h][:], ACT.Copy)
+            total = sb.tile([P, E], F32, name="total%d" % h)
+            nc.vector.tensor_tensor(total[:], pages["a", h][:], pages["b", h][:], ALU.add)
+            nc.sync.dma_start(out[h * P : (h + 1) * P, :], total[:])

@@ -46,8 +46,8 @@ def tile_list_leadboth_storeleads_one_pagetwice_kernel(
             nc.vector.memset(tile[:].bitcast(I32), 0)
             return tile
 
-        def load_scales(tile, src):
-            for q in range(QUADS):
+        def load_scales(tile, src, quads=range(QUADS)):
+            for q in quads:
                 nc.sync.dma_start(tile[32 * q : 32 * q + 4, :].bitcast(I32), src[0, 4 * q : 4 * q + 4, :].bitcast(I32))
 
         xt_s = zeroed_scales(T, "xt_s")
@@ -55,14 +55,15 @@ def tile_list_leadboth_storeleads_one_pagetwice_kernel(
         wt_s = zeroed_scales(V, "wt_s")
         wb_s = zeroed_scales(N, "wb_s")
 
-        wt_w = load_words(wt_words[0], V, U16, "wt_w")
         w2_rows = sb.tile([4, QUADS, R // 4], I32, name="w2_rows")
         nc.sync.dma_start(w2_rows[:], w2_scales[0].bitcast(I32).rearrange("(q r) c -> r q c", r=4))
+        wt_w = load_words(wt_words[0], V, U16, "wt_w")
         list1 = load_list(offs, "list1")
         list2 = load_list(offs2, "list2")
+        load_scales(xt_s, xt_scales, range(3))
         xt_w = load_words(xt_words[0].rearrange("p c r -> p (c r)"), T, U32, "xt_w")
-        load_scales(xt_s, xt_scales)
         w2_w = load_words(w2_words[0].rearrange("p c r -> p (c r)"), R, U32, "w2_w")
+        load_scales(xt_s, xt_scales, range(3, 4))
         load_scales(wt_s, wt_scales)
         list3 = load_list(offs3, "list3")
         list4 = load_list(offs4, "list4")
@@ -72,31 +73,31 @@ def tile_list_leadboth_storeleads_one_pagetwice_kernel(
         list6 = load_list(offs6, "list6")
 
         pages = {}
-        for h in range(N // P):
-            for which in "ab":
-                page = sb.tile([P, E], F32, name="page_%s%d" % (which, h))
-                nc.vector.memset(page[:], 0.0)
-                pages[which, h] = page
+        for which in "ab":
+            page = sb.tile([P, E], F32, name="page_%s0" % which)
+            nc.vector.memset(page[:], 0.0)
+            pages[which, 0] = page
 
         for q in range(QUADS):
             nc.vector.tensor_copy(w2_s[32 * q : 32 * q + 4, :].bitcast(I32), w2_rows[:, q, :])
+        w2_ds = sb.tile([P, R], U8, name="w2_ds", align_bytes=64)
+        nc.vector.tensor_copy(w2_ds[:].rearrange("p (t m) -> p t m", t=PACK), w2_s[:].rearrange("p (m t) -> p t m", t=PACK))
 
-        wt_g = sb.tile([P, R], U16, name="wt_g")
+        wt_g = sb.tile([P, R], U16, name="wt_g", align_bytes=64)
         nc.vector.tensor_copy(wt_g[:], wt_w[:].indirect(list1[:]))
-        wt_d = sb.tile([P, R], U16, name="wt_d", align_bytes=64)
-        nc.vector.tensor_copy(wt_d[:].rearrange("p (t m) -> p t m", t=PACK), wt_g[:].rearrange("p (m t) -> p t m", t=PACK))
         xt_g = sb.tile([P, J], U32, name="xt_g", align_bytes=64)
         nc.vector.tensor_copy(xt_g[:], xt_w[:].indirect(list2[:]))
         xt_gs = sb.tile([P, J], U8, name="xt_gs", align_bytes=64)
         nc.vector.tensor_copy(xt_gs[:], xt_s[:].indirect(list2[:]))
 
         w2_d = sb.tile([P, R], U32, name="w2_d", align_bytes=64)
-        nc.scalar.copy(w2_d[:].rearrange("p (t m) -> p t m", t=PACK), w2_w[:].rearrange("p (m t) -> p t m", t=PACK))
-        w2_ds = sb.tile([P, R], U8, name="w2_ds", align_bytes=64)
-        nc.gpsimd.tensor_copy(w2_ds[:].rearrange("p (t m) -> p t m", t=PACK), w2_s[:].rearrange("p (m t) -> p t m", t=PACK))
+        nc.scalar.copy(w2_d[:].rearrange("p (t m) -> p m t", t=PACK), w2_w[:].rearrange("p (m t) -> p m t", t=PACK))
 
         wt_ds = sb.tile([P, R], U8, name="wt_ds", align_bytes=64)
         nc.vector.tensor_copy(wt_ds[:].rearrange("p (t m) -> p m t", t=PACK), wt_s[:].indirect(list1[:]))
+        wt_d = sb.tile([P, R], U16, name="wt_s", align_bytes=64)
+        for t in range(PACK):
+            nc.vector.tensor_copy(wt_d[:, t * P : (t + 1) * P], wt_g[:, t::PACK])
 
         b_rows = []
         for t in range(PACK):
@@ -117,20 +118,39 @@ def tile_list_leadboth_storeleads_one_pagetwice_kernel(
             acc = ps.tile([P, J], F32, name="acc_a%d" % t)
             nc.tensor.matmul_mx(out=acc[:], lhsT=wt_d[:, cols].bitcast(E2M1), lhsT_scale=wt_ds[:, cols],
                                 rhs=xt_g[:].bitcast(E4M3), rhs_scale=xt_gs[:], start=True, stop=True)
+            if t == 0:
+                lead_a0 = sb.tile([P, 1], F32, name="lead_a0")
+                nc.vector.tensor_copy(lead_a0[:], acc[:, 0:1])
             rows = sb.tile([P, J], F32, name="a_rows%d" % t)
             nc.vector.tensor_copy(rows[:], acc[:])
             a_rows.append(rows)
-        for t in range(PACK):
-            nc.scalar.activation(first[:, t, :], a_rows[t][:].indirect(list3[:]), ACT.Copy, scale=b_rows[t][:, 0:1])
-            nc.scalar.activation(second[:, t, :], b_rows[t][:].indirect(list4[:]), ACT.Copy, scale=a_rows[t][:, 0:1])
-            nc.vector.tensor_tensor(diff[:, t, :], first[:, t, :], second[:, t, :], ALU.subtract)
 
-        hid = sb.tile([P, O, PACK], BF16, name="hid", align_bytes=64)
-        by_place = diff[:].rearrange("p t o -> p o t")
-        nc.vector.scalar_tensor_tensor(hid[:], by_place, -1.0, by_place, ALU.mult, ALU.max)
+        def look_up(t, lo, hi):
+            lead_a = lead_a0[:] if t == 0 else a_rows[t][:, 0:1]
+            entries = slice(lo // 16, hi // 16)
+            nc.scalar.activation(second[:, t, lo:hi], b_rows[t][:].indirect(list4[:, entries]), ACT.Copy, scale=lead_a)
+            nc.scalar.activation(first[:, t, lo:hi], a_rows[t][:].indirect(list3[:, entries]), ACT.Copy, scale=b_rows[t][:, 0:1])
+            nc.vector.tensor_tensor(diff[:, t, lo:hi], first[:, t, lo:hi], second[:, t, lo:hi], ALU.subtract)
+
+        halves = ((0, O // 2), (O // 2, O))
+        for t in range(PACK - 1):
+            look_up(t, 0, O)
+        for lo, hi in halves:
+            look_up(PACK - 1, lo, hi)
+
+        for which, tag in (("a", "wt_g"), ("b", "wt_ds")):
+            page = sb.tile([P, E], F32, name=tag, align_bytes=64)
+            nc.vector.memset(page[:], 0.0)
+            pages[which, 1] = page
+
         hid_w = sb.tile([P, O], U32, name="hid_w", align_bytes=64)
         hid_s = sb.tile([P, O], U8, name="hid_s", align_bytes=64)
-        nc.vector.quantize_mx(out=hid_w[:].bitcast(E4M3), scales=hid_s[:], in_=hid[:].rearrange("p o t -> p (o t)"))
+        for lo, hi in halves:
+            hid = sb.tile([P, hi - lo, PACK], BF16, name="hid%d" % lo, align_bytes=64)
+            nc.scalar.activation(hid[:].rearrange("p (c i) t -> p c t i", i=4),
+                                 diff[:, :, lo:hi].rearrange("p t (c i) -> p c t i", i=4), ACT.Abs)
+            nc.vector.quantize_mx(out=hid_w[:, lo:hi].bitcast(E4M3), scales=hid_s[:, lo:hi],
+                                  in_=hid[:].rearrange("p o t -> p (o t)"))
 
         p_rows = []
         for h in range(N // P):
@@ -147,6 +167,9 @@ def tile_list_leadboth_storeleads_one_pagetwice_kernel(
         for h in range(N // P):
             nc.vector.tensor_copy(pages["a", h][:].indirect(list5[:]), p_rows[h][:])
             nc.scalar.activation(pages["b", h][:].indirect(list6[:]), p_rows[h][:], ACT.Copy)
-            total = sb.tile([P, E], F32, name="total%d" % h)
-            nc.vector.tensor_tensor(total[:], pages["a", h][:], pages["b", h][:], ALU.add)
-            nc.sync.dma_start(out[h * P : (h + 1) * P, :], total[:])
+            pieces = 2
+            for c in range(pieces):
+                cols = slice(c * E // pieces, (c + 1) * E // pieces)
+                total = sb.tile([P, E // pieces], F32, name="total%d_%d" % (h, c))
+                nc.vector.tensor_tensor(total[:], pages["a", h][:, cols], pages["b", h][:, cols], ALU.add)
+                nc.sync.dma_start(out[h * P : (h + 1) * P, cols], total[:])

@@ -55,7 +55,7 @@ def tile_list_leadboth_storeleads_one_pagetwice_kernel(
         wt_s = zeroed_scales(V, "wt_s")
         wb_s = zeroed_scales(N, "wb_s")
 
-        w2_rows = sb.tile([4, QUADS, R // 4], I32, name="w2_rows")
+        w2_rows = sb.tile([4, QUADS, R // 4], I32, name="w2_rows", align_bytes=64)
         nc.sync.dma_start(w2_rows[:], w2_scales[0].bitcast(I32).rearrange("(q r) c -> r q c", r=4))
         wt_w = load_words(wt_words[0], V, U16, "wt_w")
         list1 = load_list(offs, "list1")
@@ -81,7 +81,11 @@ def tile_list_leadboth_storeleads_one_pagetwice_kernel(
         for q in range(QUADS):
             nc.vector.tensor_copy(w2_s[32 * q : 32 * q + 4, :].bitcast(I32), w2_rows[:, q, :])
         w2_ds = sb.tile([P, R], U8, name="w2_ds", align_bytes=64)
-        nc.vector.tensor_copy(w2_ds[:].rearrange("p (t m) -> p t m", t=PACK), w2_s[:].rearrange("p (m t) -> p t m", t=PACK))
+        nc.gpsimd.tensor_copy(w2_ds[:].rearrange("p (t m) -> p t m", t=PACK), w2_s[:].rearrange("p (m t) -> p t m", t=PACK))
+        for which, tag in (("a", "w2_rows"), ("b", "w2_s")):
+            page = sb.tile([P, E], F32, name=tag, align_bytes=64)
+            nc.gpsimd.memset(page[:], 0.0)
+            pages[which, 1] = page
 
         wt_g = sb.tile([P, R], U16, name="wt_g", align_bytes=64)
         nc.vector.tensor_copy(wt_g[:], wt_w[:].indirect(list1[:]))
@@ -137,11 +141,6 @@ def tile_list_leadboth_storeleads_one_pagetwice_kernel(
             look_up(t, 0, O)
         for lo, hi in halves:
             look_up(PACK - 1, lo, hi)
-
-        for which, tag in (("a", "wt_g"), ("b", "wt_ds")):
-            page = sb.tile([P, E], F32, name=tag, align_bytes=64)
-            nc.vector.memset(page[:], 0.0)
-            pages[which, 1] = page
 
         hid_w = sb.tile([P, O], U32, name="hid_w", align_bytes=64)
         hid_s = sb.tile([P, O], U8, name="hid_s", align_bytes=64)

from contextlib import ExitStack

import concourse.mybir as mybir

K, T, J, R, V, O, N, E = 512, 1024, 256, 512, 1024, 128, 256, 512
FLOPS = 2 * (2 * K * R * J + R * N * O)

F32 = mybir.dt.float32
BF16 = mybir.dt.bfloat16
I32 = mybir.dt.int32
U32 = mybir.dt.uint32
U16 = mybir.dt.uint16
U8 = mybir.dt.uint8
E4M3 = mybir.dt.float8_e4m3fn_x4
E5M2 = mybir.dt.float8_e5m2_x4
E2M1 = mybir.dt.float4_e2m1fn_x4
ALU = mybir.AluOpType
ACT = mybir.ActivationFunctionType

P = 128
PACK = 4
QUADS = 4


def tile_list_leadboth_storeleads_one_pagetwice_kernel(
    tc, xt_words, xt_scales, wt_words, wt_scales, w2_words, w2_scales, wb_words, wb_scales,
    offs, offs2, offs3, offs4, offs5, offs6, out,
):
    nc = tc.nc
    with ExitStack() as ctx:
        sb = ctx.enter_context(tc.tile_pool(name="sb", bufs=1))
        ps = ctx.enter_context(tc.psum_pool(name="ps", bufs=1))

        def load_list(src, name):
            tile = sb.tile([P, src.shape[1]], U16, name=name)
            nc.sync.dma_start(tile[:], src)
            return tile

        def load_words(src, cols, dtype, name):
            tile = sb.tile([P, cols], dtype, name=name, align_bytes=64)
            nc.sync.dma_start(tile[:].bitcast(I32), src.bitcast(I32))
            return tile

        def zeroed_scales(cols, name):
            tile = sb.tile([P, cols], U8, name=name, align_bytes=64)
            nc.vector.memset(tile[:].bitcast(I32), 0)
            return tile

        def load_scales(tile, src, quads=range(QUADS)):
            for q in quads:
                nc.sync.dma_start(tile[32 * q : 32 * q + 4, :].bitcast(I32), src[0, 4 * q : 4 * q + 4, :].bitcast(I32))

        xt_s = zeroed_scales(T, "xt_s")
        w2_s = zeroed_scales(R, "w2_s")
        wt_s = zeroed_scales(V, "wt_s")
        wb_s = zeroed_scales(N, "wb_s")

        w2_rows = sb.tile([4, QUADS, R // 4], I32, name="w2_rows", align_bytes=64)
        nc.sync.dma_start(w2_rows[:], w2_scales[0].bitcast(I32).rearrange("(q r) c -> r q c", r=4))
        wt_w = load_words(wt_words[0], V, U16, "wt_w")
        list1 = load_list(offs, "list1")
        list2 = load_list(offs2, "list2")
        load_scales(xt_s, xt_scales, range(3))
        xt_w = load_words(xt_words[0].rearrange("p c r -> p (c r)"), T, U32, "xt_w")
        w2_w = load_words(w2_words[0].rearrange("p c r -> p (c r)"), R, U32, "w2_w")
        load_scales(xt_s, xt_scales, range(3, 4))
        load_scales(wt_s, wt_scales)
        list3 = load_list(offs3, "list3")
        list4 = load_list(offs4, "list4")
        wb_w = load_words(wb_words[0].rearrange("p c r -> p (c r)"), N, U32, "wb_w")
        load_scales(wb_s, wb_scales)
        list5 = load_list(offs5, "list5")
        list6 = load_list(offs6, "list6")

        pages = {}
        for which in "ab":
            page = sb.tile([P, E], F32, name="page_%s0" % which)
            nc.vector.memset(page[:], 0.0)
            pages[which, 0] = page

        for q in range(QUADS):
            nc.vector.tensor_copy(w2_s[32 * q : 32 * q + 4, :].bitcast(I32), w2_rows[:, q, :])
        w2_ds = sb.tile([P, R], U8, name="w2_ds", align_bytes=64)
        nc.gpsimd.tensor_copy(w2_ds[:].rearrange("p (t m) -> p t m", t=PACK), w2_s[:].rearrange("p (m t) -> p t m", t=PACK))
        for which, tag in (("a", "w2_rows"), ("b", "w2_s")):
            page = sb.tile([P, E], F32, name=tag, align_bytes=64)
            nc.gpsimd.memset(page[:], 0.0)
            pages[which, 1] = page

        wt_g = sb.tile([P, R], U16, name="wt_g", align_bytes=64)
        nc.vector.tensor_copy(wt_g[:], wt_w[:].indirect(list1[:]))
        xt_g = sb.tile([P, J], U32, name="xt_g", align_bytes=64)
        nc.vector.tensor_copy(xt_g[:], xt_w[:].indirect(list2[:]))
        xt_gs = sb.tile([P, J], U8, name="xt_gs", align_bytes=64)
        nc.vector.tensor_copy(xt_gs[:], xt_s[:].indirect(list2[:]))

        w2_d = sb.tile([P, R], U32, name="w2_d", align_bytes=64)
        nc.scalar.copy(w2_d[:].rearrange("p (t m) -> p m t", t=PACK), w2_w[:].rearrange("p (m t) -> p m t", t=PACK))

        wt_ds = sb.tile([P, R], U8, name="wt_ds", align_bytes=64)
        nc.vector.tensor_copy(wt_ds[:].rearrange("p (t m) -> p m t", t=PACK), wt_s[:].indirect(list1[:]))
        wt_d = sb.tile([P, R], U16, name="wt_s", align_bytes=64)
        for t in range(PACK):
            nc.vector.tensor_copy(wt_d[:, t * P : (t + 1) * P], wt_g[:, t::PACK])

        b_rows = []
        for t in range(PACK):
            cols = slice(t * P, (t + 1) * P)
            acc = ps.tile([P, J], F32, name="acc_b%d" % t)
            nc.tensor.matmul_mx(out=acc[:], lhsT=w2_d[:, cols].bitcast(E5M2), lhsT_scale=w2_ds[:, cols],
                                rhs=xt_g[:].bitcast(E4M3), rhs_scale=xt_gs[:], start=True, stop=True)
            rows = sb.tile([P, J], F32, name="b_rows%d" % t)
            nc.scalar.activation(rows[:], acc[:], ACT.Copy)
            b_rows.append(rows)

        first = sb.tile([P, PACK, O], F32, name="first")
        second = sb.tile([P, PACK, O], F32, name="second")
        diff = sb.tile([P, PACK, O], F32, name="diff")
        a_rows = []
        for t in range(PACK):
            cols = slice(t * P, (t + 1) * P)
            acc = ps.tile([P, J], F32, name="acc_a%d" % t)
            nc.tensor.matmul_mx(out=acc[:], lhsT=wt_d[:, cols].bitcast(E2M1), lhsT_scale=wt_ds[:, cols],
                                rhs=xt_g[:].bitcast(E4M3), rhs_scale=xt_gs[:], start=True, stop=True)
            if t == 0:
                lead_a0 = sb.tile([P, 1], F32, name="lead_a0")
                nc.vector.tensor_copy(lead_a0[:], acc[:, 0:1])
            rows = sb.tile([P, J], F32, name="a_rows%d" % t)
            nc.vector.tensor_copy(rows[:], acc[:])
            a_rows.append(rows)

        def look_up(t, lo, hi):
            lead_a = lead_a0[:] if t == 0 else a_rows[t][:, 0:1]
            entries = slice(lo // 16, hi // 16)
            nc.scalar.activation(second[:, t, lo:hi], b_rows[t][:].indirect(list4[:, entries]), ACT.Copy, scale=lead_a)
            nc.scalar.activation(first[:, t, lo:hi], a_rows[t][:].indirect(list3[:, entries]), ACT.Copy, scale=b_rows[t][:, 0:1])
            nc.vector.tensor_tensor(diff[:, t, lo:hi], first[:, t, lo:hi], second[:, t, lo:hi], ALU.subtract)

        halves = ((0, O // 2), (O // 2, O))
        for t in range(PACK - 1):
            look_up(t, 0, O)
        for lo, hi in halves:
            look_up(PACK - 1, lo, hi)

        hid_w = sb.tile([P, O], U32, name="hid_w", align_bytes=64)
        hid_s = sb.tile([P, O], U8, name="hid_s", align_bytes=64)
        for lo, hi in halves:
            hid = sb.tile([P, hi - lo, PACK], BF16, name="hid%d" % lo, align_bytes=64)
            nc.scalar.activation(hid[:].rearrange("p (c i) t -> p c t i", i=4),
                                 diff[:, :, lo:hi].rearrange("p t (c i) -> p c t i", i=4), ACT.Abs)
            nc.vector.quantize_mx(out=hid_w[:, lo:hi].bitcast(E4M3), scales=hid_s[:, lo:hi],
                                  in_=hid[:].rearrange("p o t -> p (o t)"))

        p_rows = []
        for h in range(N // P):
            cols = slice(h * P, (h + 1) * P)
            acc = ps.tile([P, J], F32, name="acc_b%d" % h)
            nc.tensor.matmul_mx(out=acc[:, 0:O], lhsT=wb_w[:, cols].bitcast(E5M2), lhsT_scale=wb_s[:, cols],
                                rhs=hid_w[:].bitcast(E4M3), rhs_scale=hid_s[:], start=True, stop=True)
            rows = sb.tile([P, O], F32, name="p_rows%d" % h)
            if h == 0:
                nc.vector.tensor_copy(rows[:], acc[:, 0:O])
            else:
                nc.scalar.copy(rows[:], acc[:, 0:O])
            p_rows.append(rows)
        for h in range(N // P):
            nc.vector.tensor_copy(pages["a", h][:].indirect(list5[:]), p_rows[h][:])
            nc.scalar.activation(pages["b", h][:].indirect(list6[:]), p_rows[h][:], ACT.Copy)
            pieces = 2
            for c in range(pieces):
                cols = slice(c * E // pieces, (c + 1) * E // pieces)
                total = sb.tile([P, E // pieces], F32, name="total%d_%d" % (h, c))
                nc.vector.tensor_tensor(total[:], pages["a", h][:, cols], pages["b", h][:, cols], ALU.add)
                nc.sync.dma_start(out[h * P : (h + 1) * P, cols], total[:])
